import numpy as np, ml_dtypes
CORES = [0,8,16,24,32,40,48,56,64,72,80,88,96,104,112,120,128,136,144,152,160,168,176,184,192,200,208,216,224,232,240,248,256,264,272,280,288,296,304,312,320,328,336,344,352,360,368,376,384,392,400,408,416,424,432,440,448,456,464,472,480,488,496,504]
N = 64
TOK = 64
ROUTE = [[[26,36],[2,36],[7,46],[46,59],[14,41],[23,37],[4,24],[18,36],[13,60],[46,61],[4,6],[2,25],[42,53],[7,29],[28,53],[41,48],[5,62],[52,54],[50,54],[46,47],[12,30],[19,45],[25,52],[3,9],[36,59],[0,21],[34,45],[3,17],[14,41],[36,45],[47,60],[5,26],[11,41],[15,54],[30,48],[15,47],[14,50],[18,30],[47,62],[2,3],[21,43],[37,51],[24,56],[24,33],[6,32],[22,23],[25,41],[12,63],[13,36],[54,58],[1,56],[17,49],[7,10],[7,15],[43,47],[6,41],[5,10],[35,48],[2,56],[21,55],[32,40],[3,11],[26,39],[14,35]],[[13,28],[15,47],[20,58],[37,50],[44,56],[26,51],[40,49],[6,60],[3,56],[48,52],[7,18],[11,41],[14,29],[5,27],[24,57],[7,22],[4,39],[15,32],[8,19],[5,41],[15,56],[30,34],[50,61],[15,36],[8,49],[19,42],[6,39],[22,49],[37,41],[1,61],[17,19],[4,16],[24,62],[13,49],[16,53],[52,63],[7,11],[30,40],[16,53],[10,58],[41,43],[6,35],[27,44],[34,57],[4,51],[11,20],[11,30],[46,62],[14,53],[26,50],[62,63],[12,58],[6,44],[39,45],[6,50],[2,23],[5,36],[22,45],[3,61],[11,34],[4,60],[28,62],[7,61],[30,45]],[[24,28],[20,61],[23,39],[13,14],[1,26],[47,52],[21,41],[19,37],[19,41],[0,51],[3,59],[39,61],[2,29],[7,51],[10,35],[21,50],[38,62],[0,40],[21,40],[16,33],[55,63],[7,49],[35,43],[40,45],[26,50],[2,58],[3,9],[30,57],[27,36],[13,46],[53,63],[40,59],[8,28],[7,62],[20,56],[30,55],[39,42],[33,60],[46,55],[0,55],[7,32],[25,44],[27,46],[0,6],[33,41],[50,62],[6,40],[16,63],[30,34],[27,57],[8,18],[28,37],[5,16],[10,49],[38,59],[5,46],[16,23],[6,11],[49,54],[43,47],[7,55],[46,53],[13,48],[33,49]],[[7,39],[33,36],[30,51],[6,14],[1,32],[4,47],[30,41],[18,57],[11,31],[5,63],[22,36],[40,50],[10,32],[20,63],[5,42],[18,51],[12,60],[17,44],[40,48],[40,59],[25,27],[5,48],[1,37],[19,34],[26,35],[27,42],[14,39],[54,61],[10,36],[31,40],[36,45],[39,42],[57,63],[14,42],[40,55],[14,59],[15,54],[6,55],[21,54],[7,24],[54,55],[15,54],[15,45],[12,42],[16,55],[8,47],[44,63],[26,37],[9,35],[7,49],[18,23],[34,52],[43,49],[17,48],[23,57],[6,44],[21,59],[22,46],[34,49],[2,58],[27,48],[44,46],[23,49],[0,45]],[[32,60],[24,40],[13,29],[39,55],[20,54],[62,63],[0,56],[3,49],[37,58],[34,39],[21,30],[0,27],[43,60],[14,42],[8,31],[1,30],[35,51],[31,47],[26,47],[12,57],[3,36],[15,22],[19,36],[31,33],[14,31],[28,50],[3,38],[32,38],[9,38],[24,59],[4,28],[42,51],[16,19],[8,55],[12,42],[21,47],[27,56],[2,41],[22,26],[57,60],[13,20],[0,30],[9,18],[34,44],[11,12],[54,62],[2,60],[33,42],[30,59],[29,50],[1,22],[48,51],[34,46],[21,45],[13,39],[9,22],[7,23],[22,63],[33,55],[8,63],[20,53],[40,51],[33,42],[24,54]],[[49,54],[17,49],[31,33],[17,25],[1,33],[43,48],[46,55],[14,52],[54,62],[14,34],[29,47],[5,41],[13,42],[30,59],[46,48],[45,59],[39,49],[39,51],[29,51],[17,46],[38,53],[19,39],[5,9],[14,34],[9,55],[9,42],[4,47],[7,8],[18,30],[15,26],[19,32],[19,27],[12,30],[10,13],[8,32],[2,13],[40,45],[15,30],[3,46],[33,34],[51,57],[19,31],[30,36],[19,28],[55,63],[41,63],[24,51],[45,53],[25,37],[5,7],[34,41],[22,41],[41,54],[17,32],[34,59],[8,50],[35,61],[30,56],[47,57],[12,38],[16,47],[6,16],[33,37],[23,42]],[[10,31],[4,16],[35,45],[16,47],[45,52],[16,46],[21,36],[23,33],[24,46],[16,29],[10,25],[34,41],[3,60],[37,55],[6,42],[9,24],[3,38],[13,22],[6,38],[32,54],[32,57],[5,20],[40,51],[7,23],[5,14],[16,47],[18,23],[13,42],[48,49],[6,49],[53,62],[5,58],[31,49],[55,56],[23,33],[16,58],[19,60],[42,56],[16,21],[43,56],[28,58],[15,22],[50,56],[11,49],[5,9],[17,37],[30,57],[8,36],[29,49],[9,23],[17,52],[42,57],[20,36],[11,14],[40,61],[38,44],[30,48],[47,62],[9,63],[16,21],[7,25],[6,19],[0,13],[0,22]],[[9,61],[23,42],[4,18],[22,25],[23,54],[20,36],[21,53],[45,57],[36,44],[11,35],[41,51],[36,53],[7,30],[27,43],[23,58],[39,52],[37,62],[46,56],[23,62],[11,32],[12,53],[23,51],[28,46],[38,51],[16,36],[46,51],[9,45],[9,52],[14,39],[42,61],[21,34],[28,57],[2,40],[32,41],[12,27],[10,26],[16,63],[26,59],[6,45],[17,22],[10,15],[7,20],[5,49],[22,25],[34,37],[41,56],[18,47],[28,41],[3,62],[23,52],[4,31],[37,44],[15,58],[44,56],[15,29],[37,47],[22,27],[13,29],[34,35],[12,53],[15,49],[5,56],[12,30],[40,54]],[[26,56],[14,27],[52,54],[13,16],[31,35],[42,46],[18,58],[51,54],[48,59],[23,46],[40,41],[15,59],[1,33],[17,24],[49,54],[7,34],[3,55],[3,44],[20,48],[30,33],[11,57],[5,63],[5,30],[10,38],[12,14],[9,40],[36,56],[24,40],[14,30],[2,29],[18,49],[4,19],[2,58],[29,58],[29,58],[40,41],[1,2],[52,58],[58,59],[7,24],[36,48],[43,63],[34,56],[18,24],[11,48],[7,10],[18,26],[26,63],[6,45],[3,38],[7,31],[17,39],[1,42],[14,28],[2,15],[37,43],[22,55],[51,57],[34,63],[19,63],[29,57],[42,61],[11,44],[7,57]],[[5,23],[37,46],[7,53],[22,48],[32,43],[8,46],[23,42],[23,50],[50,53],[14,36],[18,24],[31,56],[1,30],[31,49],[48,52],[17,33],[24,36],[9,20],[34,52],[51,63],[6,14],[30,38],[35,50],[30,61],[32,63],[20,62],[28,53],[55,57],[17,35],[33,49],[9,58],[13,56],[44,47],[27,45],[24,61],[38,39],[3,38],[14,50],[23,43],[24,30],[8,22],[49,58],[29,39],[7,27],[17,48],[36,44],[4,23],[22,50],[44,58],[24,49],[33,61],[32,60],[17,32],[33,50],[18,34],[5,13],[29,31],[21,60],[24,32],[34,63],[31,41],[42,48],[8,24],[11,35]],[[23,39],[33,61],[39,56],[13,26],[41,49],[16,52],[27,54],[17,18],[22,40],[23,57],[57,62],[10,48],[45,63],[41,56],[8,13],[1,20],[3,37],[15,56],[10,21],[27,63],[29,59],[26,58],[1,41],[19,23],[10,33],[33,39],[20,49],[22,33],[16,52],[27,34],[55,56],[38,63],[32,46],[40,45],[21,40],[43,52],[5,14],[34,58],[11,39],[22,29],[37,45],[38,42],[11,15],[11,47],[29,49],[29,32],[45,55],[15,56],[9,49],[55,57],[16,28],[31,34],[40,44],[13,48],[26,38],[12,48],[38,58],[37,53],[14,50],[51,53],[23,40],[18,44],[34,41],[15,60]],[[20,34],[52,60],[8,15],[13,50],[20,35],[8,40],[21,57],[16,62],[18,57],[53,62],[21,27],[25,45],[44,54],[43,55],[13,28],[21,63],[23,41],[1,14],[26,61],[2,51],[36,62],[25,55],[16,46],[6,43],[7,40],[48,59],[30,62],[16,39],[42,60],[8,33],[6,33],[7,23],[41,57],[48,56],[8,32],[31,63],[12,19],[13,54],[16,56],[11,47],[34,42],[30,36],[9,50],[8,25],[3,56],[15,49],[33,62],[13,57],[22,58],[51,58],[7,25],[4,63],[35,45],[8,55],[30,37],[45,56],[48,52],[2,45],[29,53],[11,25],[26,31],[18,33],[4,59],[21,41]],[[32,60],[37,49],[36,45],[15,56],[33,63],[0,52],[2,42],[32,47],[21,57],[29,48],[38,47],[53,57],[40,55],[32,53],[40,51],[14,33],[3,8],[30,58],[29,55],[4,58],[3,4],[3,19],[4,21],[27,49],[18,27],[14,50],[38,51],[16,31],[19,50],[37,58],[25,46],[7,45],[8,15],[39,48],[42,52],[50,60],[17,38],[36,63],[8,24],[6,14],[23,31],[41,48],[27,52],[7,21],[15,38],[6,37],[6,22],[35,57],[38,48],[31,49],[17,30],[7,62],[29,36],[12,41],[8,61],[26,44],[11,36],[1,32],[43,50],[10,59],[17,48],[3,61],[37,41],[53,56]],[[24,50],[9,46],[21,33],[4,59],[7,42],[22,49],[1,36],[36,48],[4,31],[5,59],[17,22],[1,24],[37,59],[30,32],[24,46],[2,47],[10,40],[3,49],[13,31],[31,38],[25,38],[16,41],[18,58],[28,62],[6,40],[3,42],[20,49],[1,8],[50,61],[26,58],[6,40],[19,52],[12,40],[51,60],[14,45],[37,54],[2,34],[32,42],[13,44],[12,39],[8,17],[13,48],[45,60],[26,48],[28,38],[44,59],[9,45],[8,24],[17,36],[20,62],[30,52],[32,38],[48,56],[29,55],[30,60],[26,35],[8,20],[40,60],[7,33],[1,46],[6,27],[32,49],[43,53],[11,55]],[[3,31],[28,53],[0,44],[14,16],[5,6],[6,23],[38,46],[21,43],[7,35],[4,17],[8,30],[26,60],[7,52],[6,10],[32,37],[23,25],[3,27],[2,52],[25,39],[5,6],[12,58],[1,37],[0,39],[8,61],[33,56],[6,21],[40,41],[31,44],[16,19],[21,59],[44,49],[17,30],[33,55],[20,28],[40,48],[9,29],[12,50],[13,29],[26,46],[32,39],[0,28],[14,28],[35,48],[12,40],[11,39],[38,60],[0,24],[2,24],[7,52],[33,53],[49,62],[15,20],[7,41],[27,42],[19,47],[51,54],[20,40],[8,55],[40,42],[37,46],[14,37],[13,37],[8,15],[21,35]],[[10,20],[46,55],[22,41],[42,56],[31,57],[37,58],[24,25],[41,48],[18,36],[12,13],[53,55],[16,60],[20,29],[19,40],[36,39],[12,53],[28,41],[27,54],[7,39],[10,33],[24,29],[12,24],[36,61],[24,49],[35,36],[0,27],[32,41],[18,48],[5,27],[37,39],[7,14],[20,29],[47,50],[21,26],[3,56],[29,41],[3,28],[27,52],[37,57],[6,10],[12,43],[15,41],[9,35],[4,33],[24,54],[5,46],[11,39],[12,48],[33,43],[0,56],[0,28],[59,62],[44,47],[1,43],[19,25],[25,26],[14,57],[41,44],[9,10],[3,35],[45,59],[19,28],[18,61],[30,42]],[[10,23],[2,21],[19,61],[40,52],[2,7],[36,42],[52,63],[19,20],[0,20],[18,35],[17,43],[28,49],[60,63],[16,55],[4,63],[4,49],[5,13],[20,59],[15,21],[19,31],[32,63],[21,53],[13,50],[9,56],[58,61],[1,23],[0,12],[22,47],[33,50],[52,60],[19,54],[3,43],[12,58],[4,9],[33,59],[18,40],[45,58],[33,54],[24,54],[7,59],[7,44],[26,58],[36,42],[16,39],[35,45],[29,37],[16,43],[1,33],[9,63],[19,43],[37,63],[32,44],[0,40],[21,42],[42,54],[55,62],[21,40],[1,59],[22,57],[20,38],[18,47],[11,55],[1,43],[1,3]],[[20,31],[20,48],[6,47],[4,38],[6,20],[26,44],[14,56],[3,53],[18,22],[13,20],[37,50],[8,42],[22,45],[29,39],[14,54],[25,42],[8,30],[30,40],[43,46],[4,60],[5,29],[27,33],[36,49],[9,28],[24,45],[7,51],[5,27],[18,56],[50,58],[28,32],[24,26],[0,23],[16,36],[10,22],[4,34],[17,47],[15,45],[40,53],[19,55],[46,54],[18,39],[57,61],[23,42],[2,11],[1,12],[44,49],[34,51],[0,15],[28,33],[17,42],[15,41],[6,7],[2,6],[33,43],[8,37],[23,36],[4,16],[1,11],[29,63],[30,51],[25,45],[18,63],[37,59],[16,24]],[[41,54],[29,31],[58,62],[0,23],[34,62],[35,37],[57,63],[6,51],[21,45],[3,14],[21,29],[18,53],[3,49],[6,37],[31,34],[12,28],[3,52],[32,37],[8,19],[21,33],[36,52],[9,17],[20,48],[17,32],[2,9],[1,33],[4,26],[3,17],[35,52],[12,62],[14,21],[8,34],[9,56],[36,55],[45,49],[15,38],[23,40],[8,61],[14,31],[12,14],[36,46],[18,39],[7,10],[1,30],[18,61],[16,45],[0,54],[25,50],[26,48],[16,36],[37,58],[9,30],[8,40],[36,52],[36,41],[33,42],[40,41],[13,50],[29,35],[11,62],[1,15],[15,40],[35,51],[9,20]],[[39,41],[19,37],[48,63],[21,59],[22,37],[44,49],[5,18],[16,39],[13,14],[2,23],[4,12],[1,14],[46,63],[1,62],[22,35],[22,58],[2,48],[5,32],[11,35],[23,38],[10,62],[13,20],[37,53],[5,30],[14,48],[4,50],[25,63],[5,31],[0,20],[24,48],[1,40],[34,51],[40,54],[15,50],[5,61],[12,58],[24,26],[22,35],[49,60],[24,43],[32,52],[12,43],[25,41],[9,29],[25,59],[15,25],[9,23],[22,60],[16,41],[33,34],[21,63],[19,54],[6,29],[17,28],[39,41],[36,56],[8,44],[12,21],[8,13],[13,14],[5,43],[17,48],[24,42],[12,61]],[[46,53],[17,40],[29,48],[28,47],[11,53],[17,20],[0,11],[30,39],[4,17],[47,57],[40,54],[50,60],[10,34],[13,14],[5,36],[0,31],[18,43],[8,54],[54,60],[0,4],[8,40],[8,40],[28,39],[25,63],[19,20],[13,33],[14,31],[10,56],[14,60],[17,56],[15,38],[13,40],[16,33],[4,34],[21,24],[22,57],[11,22],[3,39],[20,35],[6,30],[14,29],[45,53],[27,30],[10,15],[14,44],[16,29],[28,61],[55,58],[3,31],[34,59],[44,46],[9,17],[33,60],[47,62],[48,49],[19,61],[9,45],[30,54],[8,57],[7,26],[18,57],[0,23],[23,38],[52,57]],[[17,61],[8,13],[22,23],[49,60],[37,61],[25,59],[24,47],[30,34],[4,36],[18,38],[1,56],[20,53],[0,36],[36,38],[17,33],[37,62],[15,19],[21,34],[19,25],[59,61],[56,62],[16,58],[4,12],[33,55],[22,48],[34,61],[13,48],[0,55],[3,12],[4,14],[11,43],[20,27],[11,52],[39,43],[37,49],[15,27],[2,4],[7,57],[26,62],[18,54],[8,61],[33,63],[52,63],[16,45],[44,58],[38,58],[41,60],[9,23],[16,39],[12,39],[55,61],[44,48],[18,43],[25,60],[7,40],[22,50],[19,38],[41,62],[7,38],[28,49],[6,21],[28,63],[8,46],[11,49]],[[54,57],[3,10],[57,59],[0,38],[12,13],[49,62],[39,40],[29,47],[11,52],[16,17],[4,36],[20,48],[16,47],[6,26],[4,58],[8,33],[0,21],[7,58],[39,60],[7,37],[22,60],[8,40],[33,57],[4,19],[26,49],[40,55],[16,42],[10,17],[24,62],[31,38],[0,17],[26,48],[62,63],[51,58],[13,52],[4,36],[16,56],[34,41],[27,48],[5,50],[31,53],[39,58],[37,40],[42,63],[5,47],[5,22],[0,39],[11,41],[5,49],[4,39],[53,60],[3,62],[24,25],[10,30],[40,57],[41,43],[36,62],[32,37],[16,62],[20,40],[9,52],[35,47],[4,24],[30,58]],[[5,21],[3,49],[7,18],[14,50],[13,28],[43,62],[37,54],[16,38],[31,50],[11,20],[10,40],[7,21],[39,57],[20,26],[0,50],[34,63],[11,37],[9,10],[11,17],[38,48],[41,57],[24,30],[12,33],[27,42],[20,42],[10,35],[10,40],[30,55],[15,16],[43,60],[6,59],[34,58],[35,37],[47,52],[2,46],[6,16],[41,57],[4,42],[6,60],[34,54],[46,48],[31,46],[11,26],[52,62],[56,58],[9,44],[0,27],[29,57],[35,63],[33,41],[10,57],[21,27],[29,50],[36,63],[33,43],[2,43],[22,26],[6,18],[11,24],[22,50],[16,33],[29,49],[5,25],[8,47]],[[2,27],[8,42],[20,45],[11,24],[42,52],[8,17],[20,30],[2,44],[4,27],[9,61],[18,27],[3,46],[30,41],[30,44],[14,53],[12,59],[24,36],[10,51],[39,58],[12,21],[36,53],[30,44],[0,54],[0,26],[38,46],[1,52],[19,56],[9,40],[41,51],[15,23],[21,47],[15,24],[40,60],[12,34],[5,37],[4,39],[32,60],[5,11],[18,46],[7,40],[13,48],[46,52],[4,18],[19,55],[32,53],[32,50],[14,45],[28,51],[15,60],[3,25],[41,48],[19,51],[26,41],[26,63],[45,57],[27,40],[33,62],[24,43],[17,38],[31,40],[18,24],[4,33],[3,26],[25,33]],[[50,61],[10,38],[5,10],[55,60],[43,48],[26,36],[9,25],[11,62],[32,45],[24,45],[11,59],[1,33],[34,38],[4,43],[35,50],[35,59],[13,39],[26,45],[19,25],[30,53],[51,58],[42,57],[19,54],[36,37],[19,58],[55,62],[34,47],[4,28],[62,63],[7,8],[18,49],[21,49],[7,41],[27,46],[45,56],[37,62],[4,37],[7,45],[5,17],[20,42],[1,54],[41,43],[52,59],[32,62],[8,47],[18,50],[22,59],[16,52],[46,58],[33,45],[16,50],[10,37],[25,29],[9,29],[1,46],[4,60],[27,32],[3,21],[17,53],[22,43],[13,29],[5,34],[2,24],[11,48]],[[37,43],[22,63],[33,39],[0,3],[20,53],[4,9],[28,57],[3,37],[19,50],[13,26],[0,5],[5,56],[14,37],[18,42],[5,26],[27,61],[5,37],[23,27],[14,33],[55,62],[40,54],[2,37],[32,39],[37,57],[38,39],[13,37],[39,48],[24,50],[19,55],[47,55],[24,51],[26,39],[25,38],[41,45],[3,55],[15,19],[1,45],[24,43],[28,44],[11,55],[37,39],[45,47],[34,44],[33,47],[26,32],[12,23],[9,52],[47,59],[9,10],[39,58],[22,47],[9,14],[10,30],[2,49],[7,37],[2,31],[18,60],[5,15],[45,58],[4,10],[24,47],[3,14],[46,54],[11,31]],[[50,56],[37,38],[19,55],[5,23],[23,27],[10,44],[31,63],[25,51],[27,34],[14,39],[7,20],[18,39],[15,45],[27,30],[7,55],[56,62],[0,19],[1,10],[7,34],[7,35],[32,46],[3,44],[6,15],[38,46],[57,58],[16,22],[16,58],[9,16],[2,51],[17,18],[14,27],[3,44],[4,15],[39,50],[41,46],[54,55],[21,22],[25,32],[56,63],[7,21],[21,51],[42,60],[3,60],[33,34],[16,45],[29,63],[8,62],[41,59],[27,52],[12,19],[18,39],[13,45],[38,43],[1,48],[25,61],[7,10],[23,45],[7,38],[15,39],[34,47],[17,43],[17,22],[12,13],[44,57]],[[8,23],[25,37],[26,49],[35,36],[11,15],[9,47],[0,50],[45,53],[30,42],[7,58],[9,23],[17,61],[17,56],[13,57],[36,60],[2,7],[14,29],[31,62],[13,56],[11,36],[3,36],[15,59],[39,43],[21,24],[11,62],[42,59],[34,37],[6,19],[39,43],[14,45],[22,44],[38,57],[27,30],[10,20],[0,55],[20,58],[44,55],[6,19],[27,36],[30,53],[10,22],[48,54],[30,39],[46,61],[16,45],[5,54],[58,61],[12,59],[15,51],[5,22],[29,54],[15,49],[15,44],[25,42],[25,41],[16,34],[29,55],[37,39],[1,6],[14,55],[45,62],[5,55],[12,22],[39,60]],[[7,24],[37,57],[41,62],[18,40],[44,57],[16,22],[44,53],[26,42],[42,43],[12,20],[34,36],[20,42],[14,19],[5,41],[10,12],[12,51],[10,28],[12,58],[13,28],[5,23],[13,23],[13,23],[16,34],[27,47],[17,31],[43,51],[3,18],[44,55],[41,52],[25,58],[7,62],[48,58],[10,53],[12,14],[10,55],[41,63],[11,12],[13,59],[4,13],[13,14],[22,29],[16,18],[15,40],[24,43],[54,61],[22,62],[16,40],[54,62],[22,47],[12,51],[46,60],[5,54],[0,41],[33,61],[31,63],[18,56],[16,30],[8,25],[7,43],[8,13],[16,46],[22,56],[13,58],[35,44]],[[36,57],[36,41],[16,33],[12,27],[4,50],[12,54],[8,51],[13,35],[17,39],[30,47],[9,48],[21,39],[11,52],[14,17],[20,21],[51,58],[33,44],[26,39],[26,59],[12,41],[48,60],[11,60],[36,39],[16,41],[14,32],[17,58],[21,60],[14,25],[36,52],[21,37],[25,30],[6,16],[25,60],[12,47],[3,52],[32,46],[19,49],[32,45],[8,25],[7,29],[34,42],[13,62],[5,39],[4,53],[50,56],[32,55],[39,60],[7,57],[3,41],[19,48],[43,47],[18,29],[5,31],[20,24],[18,32],[28,29],[0,23],[10,13],[0,54],[16,36],[22,58],[1,39],[7,11],[36,62]],[[6,35],[22,50],[23,31],[8,32],[24,39],[1,13],[27,51],[3,28],[7,8],[4,22],[11,38],[34,63],[19,27],[31,58],[50,53],[22,57],[4,16],[10,55],[43,56],[6,30],[5,13],[46,48],[28,59],[21,51],[40,61],[27,55],[26,39],[46,60],[23,47],[29,49],[3,60],[31,40],[5,25],[15,28],[6,24],[7,10],[30,36],[1,32],[16,25],[59,62],[23,55],[3,16],[18,21],[10,43],[7,30],[4,17],[32,59],[0,37],[44,50],[16,35],[35,51],[30,38],[44,57],[3,44],[24,61],[22,28],[3,28],[16,38],[2,5],[36,41],[38,56],[4,38],[9,36],[32,47]],[[6,46],[26,55],[7,30],[26,31],[11,28],[48,63],[0,1],[29,61],[35,49],[37,50],[43,63],[17,23],[24,63],[12,31],[7,11],[0,7],[16,30],[12,21],[30,43],[4,41],[16,31],[3,4],[15,16],[40,63],[8,38],[6,29],[36,39],[24,50],[42,48],[35,42],[33,49],[1,13],[11,58],[25,46],[3,50],[21,49],[13,41],[17,32],[39,41],[16,31],[34,57],[41,59],[37,56],[12,27],[11,14],[30,52],[19,39],[1,60],[0,48],[40,61],[3,28],[26,53],[9,54],[21,57],[29,55],[2,56],[9,45],[4,25],[4,36],[21,25],[1,16],[25,55],[18,23],[1,19]],[[28,33],[25,45],[22,31],[26,39],[41,47],[36,58],[54,57],[21,33],[29,50],[25,51],[9,19],[1,15],[24,35],[5,54],[15,38],[18,58],[34,45],[43,57],[29,57],[44,51],[13,58],[43,53],[30,43],[44,53],[3,22],[31,44],[0,24],[5,33],[12,47],[13,21],[58,60],[26,50],[28,55],[27,59],[43,57],[26,45],[7,44],[15,23],[42,58],[43,44],[20,56],[38,45],[13,47],[43,55],[46,57],[24,32],[9,42],[4,55],[26,52],[0,52],[37,54],[48,51],[19,54],[4,30],[7,38],[22,58],[22,60],[20,61],[18,20],[32,38],[13,47],[5,24],[4,5],[55,56]],[[31,38],[39,46],[29,38],[19,39],[11,48],[0,27],[9,40],[56,61],[10,49],[19,49],[14,30],[4,26],[12,62],[41,43],[3,36],[24,54],[21,28],[40,59],[34,53],[35,53],[20,29],[13,17],[60,63],[50,55],[40,62],[14,15],[26,60],[23,41],[27,42],[1,23],[50,54],[35,55],[12,27],[7,53],[34,49],[4,49],[35,37],[4,47],[3,51],[20,40],[45,46],[23,24],[11,12],[1,16],[19,50],[19,48],[26,31],[35,44],[23,45],[5,19],[7,38],[25,32],[30,33],[32,62],[57,60],[8,10],[39,61],[14,56],[34,63],[23,61],[26,42],[46,58],[32,45],[22,47]],[[24,31],[58,63],[15,43],[9,18],[1,15],[10,33],[7,46],[20,21],[3,8],[44,63],[3,37],[17,43],[22,31],[46,48],[19,58],[6,13],[5,35],[1,7],[0,14],[34,36],[2,24],[44,53],[40,51],[42,60],[41,62],[48,52],[17,63],[39,41],[5,49],[9,47],[34,41],[10,12],[5,59],[14,27],[15,26],[9,12],[6,10],[43,45],[3,21],[27,43],[16,28],[22,38],[36,58],[5,59],[9,13],[29,61],[15,40],[23,62],[17,33],[5,16],[24,31],[18,49],[19,42],[33,36],[2,22],[28,50],[16,46],[46,53],[3,36],[13,17],[3,23],[39,53],[18,47],[9,27]],[[28,37],[40,50],[38,53],[35,61],[12,36],[35,49],[13,55],[13,40],[1,16],[17,37],[21,54],[32,54],[38,43],[13,30],[23,63],[5,17],[14,37],[28,49],[26,41],[35,55],[18,28],[47,58],[12,17],[26,48],[24,50],[45,56],[20,45],[2,54],[16,60],[22,31],[16,24],[37,40],[24,33],[3,63],[11,59],[27,38],[33,46],[2,13],[30,39],[37,40],[30,48],[36,61],[17,33],[16,55],[16,34],[52,57],[8,49],[9,32],[14,23],[35,63],[47,58],[8,45],[3,24],[3,44],[30,32],[34,45],[9,21],[42,47],[9,22],[6,37],[6,58],[46,63],[40,49],[22,45]],[[18,36],[31,62],[8,40],[14,49],[0,18],[23,49],[17,45],[31,46],[16,17],[11,44],[34,55],[5,18],[26,28],[15,33],[25,49],[21,55],[11,42],[6,31],[24,39],[1,20],[25,59],[3,34],[11,51],[23,63],[10,56],[27,34],[1,36],[43,52],[56,58],[31,53],[10,32],[11,39],[3,37],[5,22],[13,17],[9,25],[42,62],[8,44],[48,59],[13,21],[14,63],[15,46],[55,59],[33,38],[9,29],[14,24],[31,55],[15,20],[36,54],[26,56],[9,27],[51,55],[25,32],[9,55],[31,47],[20,29],[22,27],[9,25],[44,51],[8,54],[17,34],[1,15],[23,57],[33,53]],[[0,11],[55,61],[45,58],[31,40],[19,22],[6,19],[24,29],[11,26],[13,39],[25,33],[3,55],[22,43],[36,41],[26,60],[37,63],[43,45],[8,10],[43,47],[47,52],[9,46],[26,40],[36,44],[24,60],[2,43],[6,26],[33,49],[30,31],[11,39],[17,47],[0,6],[47,56],[22,49],[1,44],[41,58],[6,14],[23,40],[27,43],[8,33],[23,25],[23,62],[6,33],[8,17],[5,26],[48,49],[11,58],[35,47],[19,44],[23,46],[29,58],[12,52],[38,47],[29,41],[37,54],[18,62],[44,48],[39,43],[39,41],[39,60],[10,55],[2,54],[11,33],[11,26],[7,52],[15,35]],[[31,37],[36,54],[39,62],[10,31],[12,25],[43,56],[28,58],[21,24],[16,47],[14,42],[17,63],[25,52],[23,40],[9,17],[23,45],[41,58],[18,38],[3,21],[54,61],[38,46],[51,59],[8,51],[35,54],[9,44],[31,47],[21,52],[4,47],[34,36],[33,52],[33,42],[7,43],[12,43],[20,22],[18,61],[30,55],[47,61],[0,47],[9,22],[11,22],[18,26],[32,41],[16,18],[3,54],[6,16],[33,37],[33,57],[33,55],[58,59],[4,32],[5,48],[7,46],[12,58],[47,63],[18,44],[31,63],[25,51],[19,28],[34,50],[5,17],[17,50],[7,53],[24,49],[7,14],[16,60]],[[4,30],[2,32],[17,20],[19,23],[2,11],[5,16],[16,24],[23,34],[26,47],[1,48],[11,56],[10,40],[35,60],[35,43],[25,28],[2,33],[21,61],[62,63],[13,17],[0,60],[32,58],[23,36],[24,36],[13,33],[32,45],[2,10],[8,25],[10,25],[52,57],[17,56],[21,63],[43,62],[9,35],[16,48],[37,58],[35,56],[0,31],[1,48],[53,54],[31,46],[15,37],[0,1],[56,61],[47,49],[22,38],[41,53],[14,23],[29,57],[11,55],[18,44],[2,35],[14,47],[10,60],[18,33],[41,49],[0,24],[17,40],[11,47],[31,33],[2,53],[29,55],[40,41],[46,53],[6,37]],[[38,54],[30,56],[12,26],[33,47],[27,59],[6,35],[0,10],[52,58],[18,35],[0,17],[48,58],[43,49],[28,34],[35,63],[8,40],[46,51],[5,18],[8,48],[52,59],[40,45],[5,19],[24,42],[19,54],[18,27],[38,53],[29,46],[12,13],[22,27],[20,32],[19,51],[19,51],[51,52],[11,31],[28,39],[54,59],[38,55],[45,56],[13,14],[9,36],[2,58],[6,9],[55,56],[33,59],[5,41],[7,59],[4,59],[9,50],[0,22],[26,63],[26,45],[24,48],[30,49],[15,33],[53,62],[2,54],[14,19],[5,52],[32,43],[22,53],[32,44],[2,7],[6,37],[24,33],[27,47]],[[12,39],[41,58],[8,38],[54,62],[14,21],[37,49],[33,57],[15,59],[7,60],[8,27],[5,43],[46,56],[2,54],[12,13],[54,60],[42,44],[5,49],[27,35],[48,50],[11,12],[38,61],[16,18],[11,23],[6,53],[9,51],[16,34],[58,60],[0,56],[11,21],[20,57],[2,8],[36,50],[47,48],[0,59],[12,25],[23,37],[6,56],[11,63],[25,26],[13,49],[21,63],[5,47],[35,42],[5,41],[35,39],[8,41],[45,54],[4,41],[24,39],[8,54],[13,17],[35,51],[26,58],[55,59],[24,51],[1,61],[25,40],[41,44],[33,61],[10,11],[54,62],[5,28],[16,52],[9,38]],[[9,62],[16,25],[17,53],[7,14],[34,61],[11,37],[25,46],[30,40],[4,34],[18,31],[35,47],[22,41],[8,47],[29,37],[4,7],[2,8],[2,31],[59,61],[3,47],[48,61],[26,41],[12,27],[28,53],[4,10],[44,48],[28,62],[13,44],[2,47],[26,36],[5,58],[11,39],[38,40],[9,32],[10,47],[5,55],[36,37],[35,49],[27,34],[4,13],[16,44],[19,55],[28,51],[22,28],[6,27],[17,51],[49,62],[22,37],[32,63],[4,58],[2,48],[7,48],[3,13],[25,57],[4,13],[5,29],[14,35],[11,33],[46,57],[11,12],[4,41],[14,37],[33,36],[5,20],[54,60]],[[10,48],[32,55],[2,11],[3,24],[23,60],[9,45],[19,48],[42,54],[6,18],[22,53],[38,49],[27,32],[25,44],[3,5],[8,24],[26,42],[16,20],[19,22],[36,43],[7,60],[6,49],[24,54],[10,53],[23,55],[36,40],[25,33],[7,16],[27,43],[16,61],[3,29],[30,36],[35,57],[9,20],[3,48],[42,48],[13,52],[10,50],[5,43],[5,26],[44,62],[52,55],[9,32],[12,26],[13,32],[31,52],[33,53],[30,51],[33,47],[2,32],[41,61],[15,53],[11,55],[5,24],[42,45],[3,48],[13,14],[19,56],[1,59],[39,52],[12,15],[36,47],[1,22],[8,57],[30,49]],[[12,60],[1,20],[57,62],[28,55],[2,46],[10,46],[26,54],[40,59],[25,63],[37,40],[10,43],[0,52],[27,58],[18,24],[13,31],[41,46],[1,51],[22,25],[16,25],[4,48],[18,20],[6,36],[29,37],[21,43],[7,29],[45,46],[33,59],[15,30],[49,59],[42,54],[6,19],[28,62],[21,53],[53,57],[2,34],[4,33],[11,42],[33,48],[8,11],[33,40],[36,52],[2,57],[0,16],[38,51],[24,61],[23,33],[7,23],[48,58],[0,15],[50,59],[8,47],[19,47],[16,55],[58,63],[50,63],[30,53],[14,62],[14,24],[5,12],[24,36],[26,50],[8,53],[0,42],[52,58]],[[2,30],[49,54],[8,37],[33,54],[29,31],[11,32],[15,39],[5,37],[0,4],[27,49],[31,33],[31,55],[3,26],[3,50],[19,28],[22,57],[29,48],[50,54],[46,61],[32,59],[12,44],[1,11],[18,44],[4,55],[35,59],[7,41],[22,37],[15,50],[42,61],[28,55],[26,63],[24,27],[1,24],[36,43],[29,32],[11,50],[58,62],[59,62],[12,57],[13,50],[51,60],[44,56],[7,48],[4,47],[4,36],[2,39],[58,62],[4,30],[2,8],[7,21],[24,51],[23,38],[9,33],[4,55],[2,37],[22,50],[2,42],[5,24],[37,38],[4,36],[27,42],[30,47],[1,49],[45,57]],[[14,22],[15,24],[9,18],[31,46],[48,56],[27,50],[11,18],[5,11],[27,46],[15,39],[28,42],[2,60],[31,33],[35,55],[38,53],[11,48],[2,32],[17,38],[24,62],[17,34],[14,52],[12,20],[19,34],[15,19],[7,11],[26,57],[5,37],[10,38],[6,19],[34,35],[1,30],[15,63],[33,62],[9,28],[30,44],[23,53],[6,36],[21,47],[24,36],[25,52],[44,60],[39,43],[42,55],[35,59],[12,55],[7,29],[20,59],[1,27],[9,36],[44,48],[12,23],[18,47],[5,61],[49,63],[57,58],[20,54],[2,46],[14,48],[7,38],[6,39],[32,35],[19,21],[32,36],[8,29]],[[34,50],[55,59],[11,40],[16,51],[15,20],[27,40],[0,43],[18,38],[0,39],[7,50],[44,61],[8,30],[39,42],[35,38],[31,43],[11,26],[49,51],[24,44],[8,49],[21,58],[2,28],[23,31],[29,48],[10,59],[24,63],[1,23],[2,47],[14,17],[18,25],[48,51],[14,32],[13,36],[33,61],[45,54],[16,41],[4,54],[15,36],[13,34],[14,24],[46,49],[40,41],[47,59],[17,40],[48,54],[23,35],[10,29],[1,44],[19,63],[24,56],[16,17],[23,55],[38,56],[18,53],[7,36],[0,38],[25,53],[1,55],[18,22],[34,56],[27,36],[46,48],[7,46],[10,38],[13,29]],[[2,34],[37,52],[25,62],[6,58],[14,40],[5,54],[6,62],[10,49],[27,29],[6,29],[13,63],[4,21],[37,40],[11,18],[31,50],[7,33],[7,9],[9,39],[9,42],[4,34],[10,30],[11,18],[16,23],[42,47],[1,56],[21,29],[1,41],[48,62],[28,40],[44,63],[22,49],[12,26],[19,31],[35,58],[0,54],[51,60],[53,61],[38,60],[9,18],[13,20],[11,63],[4,15],[2,25],[58,60],[48,51],[32,54],[29,46],[16,28],[20,39],[1,4],[21,24],[12,50],[1,36],[10,20],[29,50],[29,47],[2,16],[21,35],[28,55],[22,61],[16,43],[7,8],[9,53],[5,40]],[[0,35],[49,60],[22,35],[11,14],[9,15],[12,46],[0,26],[44,61],[31,39],[44,53],[6,18],[2,36],[11,37],[0,28],[17,61],[35,49],[13,50],[5,53],[35,55],[4,47],[12,20],[17,55],[15,20],[47,62],[14,18],[33,49],[4,12],[25,47],[8,57],[13,38],[37,41],[29,58],[17,54],[27,42],[40,62],[6,25],[0,60],[19,25],[4,5],[8,45],[9,63],[46,51],[1,31],[4,46],[44,57],[43,52],[27,45],[28,37],[12,36],[7,23],[13,63],[43,63],[4,52],[21,54],[29,43],[34,53],[0,13],[23,31],[17,42],[21,53],[40,48],[45,49],[7,15],[28,54]],[[15,52],[27,41],[6,18],[23,48],[31,49],[1,35],[6,35],[9,20],[33,62],[49,61],[32,55],[47,54],[11,44],[34,43],[21,57],[6,41],[2,26],[11,22],[0,26],[27,47],[42,62],[3,5],[23,49],[59,61],[22,31],[42,50],[14,31],[53,57],[12,47],[16,22],[15,34],[7,8],[19,62],[35,46],[2,25],[26,36],[25,45],[7,36],[4,7],[13,31],[4,14],[15,47],[37,61],[10,16],[16,52],[20,45],[18,44],[8,56],[0,11],[13,58],[9,30],[10,26],[1,39],[47,52],[12,32],[14,50],[19,43],[19,35],[5,25],[15,23],[39,47],[6,32],[35,37],[22,49]],[[22,33],[1,17],[1,24],[29,62],[18,60],[6,13],[7,20],[34,38],[23,32],[48,60],[49,51],[4,41],[39,48],[18,31],[53,57],[8,46],[5,23],[13,21],[32,38],[0,46],[25,54],[12,47],[24,58],[0,1],[38,57],[0,20],[9,31],[38,56],[4,52],[18,22],[3,18],[18,32],[17,25],[1,63],[20,51],[6,62],[34,48],[23,42],[22,25],[8,33],[15,33],[36,59],[18,24],[37,54],[1,52],[12,16],[11,16],[3,50],[1,5],[1,30],[13,17],[36,45],[0,51],[2,3],[16,51],[21,56],[0,17],[51,52],[16,62],[14,60],[39,42],[12,42],[14,62],[16,17]],[[16,31],[22,25],[1,18],[0,6],[28,54],[0,63],[41,51],[32,53],[12,51],[1,38],[24,49],[1,11],[46,48],[16,51],[8,50],[11,17],[39,58],[32,38],[30,57],[46,53],[11,19],[58,62],[25,41],[17,54],[26,51],[13,26],[6,15],[5,56],[0,15],[7,18],[11,22],[44,51],[27,31],[10,29],[3,25],[6,25],[24,48],[3,10],[4,40],[14,53],[41,60],[15,40],[1,3],[51,61],[26,29],[40,54],[24,26],[13,60],[28,50],[3,38],[12,18],[52,62],[43,54],[20,36],[21,31],[15,23],[29,45],[28,40],[46,51],[3,5],[47,59],[42,54],[5,38],[50,59]],[[23,33],[15,51],[6,34],[6,14],[21,28],[50,54],[43,45],[21,30],[12,56],[10,39],[1,59],[57,62],[20,54],[4,47],[3,9],[7,37],[8,61],[52,55],[9,22],[51,59],[41,42],[29,49],[22,42],[21,29],[15,44],[38,63],[3,22],[2,35],[5,18],[22,53],[24,35],[40,45],[0,30],[8,38],[31,37],[20,52],[39,49],[45,50],[29,63],[5,18],[42,63],[7,27],[3,30],[50,55],[37,54],[21,46],[17,44],[40,48],[20,46],[21,25],[5,26],[21,25],[18,26],[7,23],[31,50],[38,48],[9,47],[10,32],[18,45],[14,24],[26,27],[2,41],[6,7],[18,59]],[[17,51],[22,55],[18,48],[4,22],[41,61],[28,47],[16,49],[33,57],[2,12],[30,56],[40,50],[14,44],[21,45],[24,40],[18,20],[10,13],[6,62],[19,26],[27,62],[16,43],[2,25],[3,25],[4,31],[19,60],[5,55],[32,40],[37,62],[3,4],[14,34],[42,49],[16,42],[29,31],[8,55],[11,17],[3,39],[35,63],[14,62],[7,19],[13,42],[17,29],[9,49],[0,1],[51,52],[1,39],[5,45],[5,31],[17,55],[22,56],[23,31],[7,60],[6,46],[32,59],[43,50],[9,49],[39,62],[36,42],[47,60],[23,53],[58,60],[18,47],[26,60],[2,49],[27,63],[0,18]],[[29,51],[3,52],[24,45],[32,51],[21,45],[40,49],[29,35],[0,50],[23,46],[18,20],[0,62],[11,26],[15,30],[39,40],[44,54],[7,12],[33,45],[10,43],[38,43],[30,63],[5,12],[38,53],[42,50],[25,59],[44,60],[2,30],[39,59],[31,49],[12,45],[7,39],[33,50],[31,37],[9,54],[39,55],[5,25],[22,58],[3,30],[2,61],[55,60],[24,29],[0,4],[28,36],[29,46],[47,54],[31,44],[40,47],[27,32],[31,46],[46,47],[14,39],[17,45],[9,42],[17,58],[18,37],[17,57],[26,41],[44,57],[26,61],[29,31],[31,58],[32,49],[27,57],[14,48],[1,4]],[[15,53],[28,50],[3,51],[2,62],[1,17],[36,49],[45,63],[16,52],[1,56],[17,39],[18,46],[24,33],[7,57],[19,30],[7,56],[11,56],[10,52],[26,40],[27,33],[11,63],[29,37],[40,48],[0,26],[54,57],[8,10],[3,29],[15,18],[27,38],[21,29],[33,51],[10,34],[24,37],[22,50],[43,62],[24,59],[9,61],[3,5],[9,30],[19,28],[5,45],[4,11],[20,44],[52,54],[11,41],[11,17],[34,35],[49,50],[23,33],[27,38],[1,12],[1,35],[36,37],[11,39],[13,44],[5,26],[46,62],[4,5],[15,55],[34,52],[22,28],[58,60],[45,63],[3,55],[16,39]],[[36,39],[37,56],[16,62],[18,39],[3,33],[39,63],[1,45],[45,63],[35,44],[48,54],[4,38],[4,43],[26,51],[22,32],[7,56],[45,55],[25,56],[11,29],[19,20],[7,54],[47,49],[40,53],[22,29],[30,51],[5,33],[1,43],[20,48],[18,23],[38,56],[30,63],[5,25],[1,7],[0,6],[6,60],[11,60],[25,39],[5,23],[6,55],[25,52],[27,31],[19,58],[6,63],[8,33],[33,40],[18,44],[20,53],[24,60],[30,34],[1,21],[21,30],[48,57],[40,44],[30,58],[11,24],[3,40],[24,33],[5,25],[9,61],[29,33],[10,24],[36,52],[45,61],[25,27],[38,43]],[[26,38],[23,38],[23,54],[49,62],[4,56],[0,63],[25,27],[12,45],[14,26],[13,14],[21,42],[5,44],[49,63],[2,36],[2,36],[23,56],[34,41],[4,33],[27,33],[9,40],[1,37],[35,47],[11,62],[9,39],[33,57],[32,55],[15,56],[27,53],[1,36],[19,51],[26,29],[8,35],[41,51],[42,58],[0,6],[0,5],[34,47],[61,62],[23,46],[26,28],[9,57],[20,48],[25,59],[23,35],[33,56],[14,23],[34,50],[4,39],[13,38],[33,57],[24,60],[0,49],[12,48],[22,42],[13,50],[29,35],[28,55],[39,48],[48,59],[11,43],[31,58],[26,34],[19,62],[10,13]],[[39,41],[1,13],[40,57],[15,28],[3,51],[0,63],[8,48],[7,8],[47,52],[58,61],[38,51],[14,24],[33,52],[5,8],[54,55],[29,59],[5,51],[26,27],[11,59],[0,28],[12,21],[38,42],[1,51],[0,61],[47,62],[25,57],[22,51],[20,47],[26,49],[4,48],[20,45],[35,53],[15,40],[45,58],[16,52],[6,37],[8,35],[42,49],[5,51],[7,58],[15,57],[3,46],[22,41],[39,44],[36,61],[21,28],[4,5],[22,42],[4,61],[18,20],[11,33],[13,40],[18,28],[30,59],[58,60],[37,39],[47,61],[45,61],[5,57],[52,57],[6,10],[0,59],[22,47],[45,50]],[[13,24],[29,58],[37,57],[16,37],[39,62],[1,29],[21,42],[12,28],[22,32],[3,62],[27,61],[50,57],[25,28],[32,43],[0,29],[20,42],[4,53],[0,23],[17,58],[18,25],[12,31],[55,59],[48,60],[26,61],[4,33],[23,46],[4,37],[26,46],[47,52],[51,59],[49,62],[31,49],[4,57],[21,42],[23,24],[34,48],[20,51],[2,15],[38,53],[39,46],[37,39],[59,62],[23,45],[16,38],[43,62],[36,39],[24,41],[38,45],[40,54],[60,62],[46,50],[23,35],[3,48],[2,38],[35,49],[22,31],[30,60],[29,49],[11,43],[20,24],[33,50],[17,50],[14,49],[4,27]],[[1,36],[34,40],[43,44],[27,57],[6,48],[32,51],[19,50],[33,39],[0,11],[3,56],[20,56],[5,32],[40,47],[5,23],[10,57],[5,38],[34,58],[59,61],[2,7],[20,27],[15,59],[2,45],[18,23],[3,5],[52,54],[5,20],[12,28],[40,49],[10,24],[9,13],[0,43],[62,63],[11,44],[28,50],[3,24],[12,36],[28,35],[26,45],[22,57],[2,14],[52,58],[4,7],[6,37],[47,52],[7,8],[54,58],[22,29],[12,38],[36,53],[16,38],[9,45],[15,63],[30,36],[29,30],[54,55],[23,48],[6,57],[41,54],[7,27],[32,59],[13,45],[5,63],[13,53],[0,22]],[[40,52],[19,40],[12,51],[30,35],[0,42],[27,50],[14,41],[7,10],[20,45],[12,61],[2,30],[27,58],[42,48],[0,46],[27,41],[37,56],[6,19],[5,41],[7,26],[15,26],[3,58],[3,24],[9,16],[35,43],[8,17],[26,28],[28,47],[28,45],[9,30],[2,37],[0,63],[9,19],[4,10],[30,36],[11,26],[21,24],[29,59],[21,57],[31,60],[7,41],[13,20],[7,46],[23,45],[6,28],[18,42],[13,50],[14,27],[6,49],[28,37],[32,55],[15,43],[15,28],[36,53],[2,13],[4,47],[32,47],[14,52],[5,23],[34,56],[13,39],[54,62],[12,15],[12,55],[13,33]]]
def setup_inputs(rng):
    return {"x": rng.standard_normal((N, 128, TOK), dtype=np.float32).astype(ml_dtypes.bfloat16), "w": rng.standard_normal((N, 128, 128), dtype=np.float32).astype(ml_dtypes.bfloat16)}
def reference(x, w):
    X, W = x.astype(np.float64), w.astype(np.float64)
    y = np.zeros((N, 128, TOK))
    for r in range(N):
        for t in range(TOK):
            for e in ROUTE[r][t]:
                y[r][:, t] += W[e].T @ X[r][:, t]
    return {"y": y.astype(ml_dtypes.bfloat16 if x.dtype != np.float64 else np.float64)}

@@ -1,0 +1,221 @@
+from concourse.bass import RemoteDMATransfer, DstId
+from concourse.mybir import AluOpType
+
+NR = 64
+LMAX = 160
+LAND = 488
+RES = 480
+
+SCRATCH = {
+    "xs": ("sbuf", [128, 64], "bfloat16"),
+    "ws": ("sbuf", [128, 128], "bfloat16"),
+    "send": ("sbuf", [128, 128], "bfloat16"),
+    "rsend": ("sbuf", [128, 128], "bfloat16"),
+    "land": ("sbuf", [128, LAND], "bfloat16"),
+    "acc": ("psum", [128, LMAX], "float32"),
+    "outb": ("sbuf", [128, LMAX], "bfloat16"),
+    "routb": ("sbuf", [128, LMAX], "bfloat16"),
+    "res": ("sbuf", [128, RES], "bfloat16"),
+    "ys": ("sbuf", [128, 64], "bfloat16"),
+}
+SEMAPHORES = ["ldx", "ldw", "packed", "blk1", "tok_in", "mm", "cast", "blk2", "res_in", "added", "stored", "sent"]
+
+
+def deal(table, same, entries, quota):
+    i = 0
+    for agent, n in quota:
+        for e in entries[i:i + n]:
+            table[(same,) + e] = agent
+        i += n
+    assert i == len(entries)
+
+
+def agent_table():
+    tab = {}
+    inter = [(k % 2, k // 2) for k in range(16)]
+    deal(tab, True, inter[1:], [(1, 9), (2, 1), (3, 1), (5, 4)])
+    deal(tab, True, [(2, k) for k in range(8)], [(5, 5), (4, 1), (6, 1), (7, 1)])
+    deal(tab, False, inter, [(2, 6), (3, 6), (7, 4)])
+    deal(tab, False, [(2, k) for k in range(8)], [(2, 2), (3, 2), (7, 4)])
+    deal(tab, True, [(3, k) for k in range(8)], [(4, 8)])
+    deal(tab, False, [(3, k) for k in range(8)], [(6, 8)])
+    return tab
+
+
+AGENT = agent_table()
+
+
+def agent_of(s, d):
+    hs, cs, hd, cd = s // 16, s % 16, d // 16, d % 16
+    if hd == hs:
+        rel = 0
+    elif hd == hs ^ 1:
+        rel = 1
+    elif hd == 3 - hs:
+        rel = 2
+    else:
+        rel = 3
+    same = (cs % 2) == (cd % 2)
+    k = (((cd - cs) if same else (cd - (cs ^ 1))) // 2) % 8
+    a = AGENT[(same, rel, k)]
+    if rel == 3:
+        return True, ((3 - hs) * 16 + cs) * 8 + a
+    return False, s * 8 + a
+
+
+def layout(s, count):
+    groups = {}
+    for d in range(NR):
+        if d != s and count[d] > 0:
+            groups.setdefault(agent_of(s, d), []).append(d)
+    sections, col, c = [], {}, 0
+    for key in sorted(groups):
+        first, msgs = c, []
+        for d in groups[key]:
+            msgs.append((d, c, count[d]))
+            col[d] = c
+            c += count[d]
+        sections.append((key[0], key[1], first, c, msgs))
+    col[s] = c
+    return {"sections": sections, "col": col, "width": c + count[s]}
+
+
+def slots(me, count):
+    at, c = {}, 0
+    for s in range(NR):
+        if s != me and count[s] > 0:
+            at[s] = c
+            c += (count[s] + 7) // 8 * 8
+    return at, c
+
+
+def make_plan(route):
+    toks = [[[] for e in range(NR)] for r in range(NR)]
+    for r in range(NR):
+        for t, pair in enumerate(route[r]):
+            for e in pair:
+                toks[r][e].append(t)
+    n = [[len(toks[r][e]) for e in range(NR)] for r in range(NR)]
+    lay1 = [layout(r, n[r]) for r in range(NR)]
+    lay2 = [layout(e, [n[r][e] for r in range(NR)]) for e in range(NR)]
+    assert max(l["width"] for l in lay2) <= LMAX and all(l["width"] == 128 for l in lay1)
+    slot1 = [slots(e, [n[r][e] for r in range(NR)]) for e in range(NR)]
+    slot2 = [slots(r, n[r]) for r in range(NR)]
+    assert max(w for at, w in slot1) <= LAND and max(w for at, w in slot2) <= RES
+    jobs = [{}, {}]
+    for ph, lays in enumerate((lay1, lay2)):
+        for s in range(NR):
+            for (relayed, core, a, b, msgs) in lays[s]["sections"]:
+                jobs[ph].setdefault(core, []).append((relayed, s, msgs))
+    return {"toks": toks, "n": n, "lay1": lay1, "lay2": lay2, "jobs": jobs,
+            "slot1": [at for at, w in slot1], "slot2": [at for at, w in slot2]}
+
+
+PLANS = {}
+
+
+def get_plan(route):
+    if "p" not in PLANS:
+        PLANS["p"] = make_plan(route)
+    return PLANS["p"]
+
+
+def emit(g, core, topo, T, writes):
+    by_width = {}
+    for w in writes:
+        by_width.setdefault(w[4], []).append(w)
+    for width in sorted(by_width):
+        ws = by_width[width]
+        for i in range(0, len(ws), 8):
+            chunk = ws[i:i + 8]
+            if len(chunk) == 1:
+                src, dst, dcore, sem, wd = chunk[0]
+                rid, pid = topo.addr(dcore, core)
+                g.remote_dma(out_ap=dst, in_ap=src, remote_sem=sem, local_sem=T.sem.sent, pid=pid, routing_id=rid,
+                             dma_engine_mask=1)
+                continue
+            trs = []
+            for j, (src, dst, dcore, sem, wd) in enumerate(chunk):
+                rid, pid = topo.addr(dcore, core)
+                trs.append(RemoteDMATransfer(dst_ids=[DstId(rid=rid, pnc=pid)], dma_engine_mask=1 << j, remote_sem=sem,
+                                             src=src, dst=dst))
+            g.remote_dma_fused(trs, local_sem=T.sem.sent)
+    return len(writes)
+
+
+def agent_program(g, core, T, topo, P):
+    sent = 0
+    for ph in (0, 1):
+        jobs = P["jobs"][ph].get(core, [])
+        if not jobs:
+            continue
+        g.wait_ge(T.sem.blk1 if ph == 0 else T.sem.blk2, len(jobs))
+        writes = []
+        for (relayed, s, msgs) in jobs:
+            if ph == 0:
+                buf, out, sem = (T.rsend if relayed else T.send), T.land, T.sem.tok_in
+            else:
+                buf, out, sem = (T.routb if relayed else T.outb), T.res, T.sem.res_in
+            for (d, c, n) in msgs:
+                at = (P["slot1"] if ph == 0 else P["slot2"])[d][s]
+                writes.append((buf[:, c:c + n], out[:, at:at + n], d * 8, sem, n))
+        sent += emit(g, core, topo, T, writes)
+    if sent:
+        g.wait_ge(T.sem.sent, sent)
+
+
+def blocks(lay, own, relay, sem):
+    return [(own[:, a:b], (relay if relayed else own)[:, a:b], core, sem, b - a)
+            for (relayed, core, a, b, msgs) in lay["sections"]]
+
+
+def rank_program(g, core, T, topo):
+    route = T.tables["ROUTE"]
+    P = get_plan(route)
+    r = T.rank_of(core)
+    if r is None:
+        agent_program(g, core, T, topo, P)
+        return
+    S, V, TE = T.sem, g.vector, g.tensor
+    l1, l2, n, toks = P["lay1"][r], P["lay2"][r], P["n"], P["toks"]
+    g.dma_start(T.xs[:], T.x[:]).then_inc(S.ldx, 16)
+    g.dma_start(T.ws[:], T.w[:]).then_inc(S.ldw, 16)
+
+    V.wait_ge(S.ldx, 16)
+    n_pack = 128 - n[r][r]
+    for e in range(NR):
+        for i, t in enumerate(toks[r][e] if e != r else []):
+            c = l1["col"][e] + i
+            V.tensor_copy(T.send[:, c:c + 1], T.xs[:, t:t + 1]).then_inc(S.packed, 1)
+    g.wait_ge(S.packed, n_pack)
+    sent = emit(g, core, topo, T, blocks(l1, T.send, T.rsend, S.blk1))
+
+    senders = [s for s in range(NR) if s != r and n[s][r]]
+    W = l2["width"]
+    TE.wait_ge(S.ldw, 16)
+    TE.wait_ge(S.ldx, 16)
+    TE.wait_ge(S.tok_in, len(senders))
+    for s in senders:
+        a, c, k = P["slot1"][r][s], l2["col"][s], n[s][r]
+        TE.matmul(T.acc[:, c:c + k], T.ws[:], T.land[:, a:a + k], True, True).then_inc(S.mm, 1)
+    for i, t in enumerate(toks[r][r]):
+        c = l2["col"][r] + i
+        TE.matmul(T.acc[:, c:c + 1], T.ws[:], T.xs[:, t:t + 1], True, True).then_inc(S.mm, 1)
+    V.wait_ge(S.mm, len(senders) + n[r][r])
+    V.tensor_copy(T.outb[:, 0:W], T.acc[:, 0:W]).then_inc(S.cast, 1)
+    g.wait_ge(S.cast, 1)
+    sent += emit(g, core, topo, T, blocks(l2, T.outb, T.routb, S.blk2))
+
+    n_back = sum(1 for e in range(NR) if e != r and n[r][e])
+    V.wait_ge(S.cast, 1)
+    V.wait_ge(S.res_in, n_back)
+    for t, pair in enumerate(route[r]):
+        ins = []
+        for e in pair:
+            c = (l2["col"][r] if e == r else P["slot2"][r][e]) + toks[r][e].index(t)
+            ins.append((T.outb if e == r else T.res)[:, c:c + 1])
+        V.tensor_tensor(T.ys[:, t:t + 1], ins[0], ins[1], AluOpType.add).then_inc(S.added, 1)
+    g.wait_ge(S.added, 64)
+    g.dma_start(T.y[:], T.ys[:]).then_inc(S.stored, 16)
+    g.wait_ge(S.stored, 16)
+    g.wait_ge(S.sent, sent)

@@ -2,113 +2,181 @@ from concourse.bass import RemoteDMATransfer, DstId
 from concourse.mybir import AluOpType
 
 NR = 64
-LMAX = 160
-LAND = 488
-RES = 480
+MATE_PORT = (2, 3, 6, 7)
+AGENTS = (4, 5, 3, 7)
+SEND, LMAX, LAND, RES, PSEND, POUT = 120, 160, 600, 392, 40, 24
 
 SCRATCH = {
     "xs": ("sbuf", [128, 64], "bfloat16"),
     "ws": ("sbuf", [128, 128], "bfloat16"),
-    "send": ("sbuf", [128, 128], "bfloat16"),
-    "rsend": ("sbuf", [128, 128], "bfloat16"),
+    "send": ("sbuf", [128, SEND], "bfloat16"),
+    "rsend": ("sbuf", [128, SEND], "bfloat16"),
+    "psend": ("sbuf", [128, PSEND], "bfloat16"),
     "land": ("sbuf", [128, LAND], "bfloat16"),
     "acc": ("psum", [128, LMAX], "float32"),
     "outb": ("sbuf", [128, LMAX], "bfloat16"),
-    "routb": ("sbuf", [128, LMAX], "bfloat16"),
+    "pout": ("sbuf", [128, POUT], "bfloat16"),
     "res": ("sbuf", [128, RES], "bfloat16"),
     "ys": ("sbuf", [128, 64], "bfloat16"),
 }
-SEMAPHORES = ["ldx", "ldw", "packed", "blk1", "tok_in", "mm", "cast", "blk2", "res_in", "added", "stored", "sent"]
+SEMAPHORES = ["ldx", "ldw", "packed", "blk1", "pblk1", "repacked", "tok_in", "mm", "cast", "blk2", "pres_in", "summed",
+              "res_in", "added", "stored", "sent"]
 
 
-def deal(table, same, entries, quota):
-    i = 0
-    for agent, n in quota:
-        for e in entries[i:i + n]:
-            table[(same,) + e] = agent
-        i += n
-    assert i == len(entries)
+def proxy_chip(r):
+    return (3 - r // 16) * 16 + r % 16
 
 
-def agent_table():
-    tab = {}
-    inter = [(k % 2, k // 2) for k in range(16)]
-    deal(tab, True, inter[1:], [(1, 9), (2, 1), (3, 1), (5, 4)])
-    deal(tab, True, [(2, k) for k in range(8)], [(5, 5), (4, 1), (6, 1), (7, 1)])
-    deal(tab, False, inter, [(2, 6), (3, 6), (7, 4)])
-    deal(tab, False, [(2, k) for k in range(8)], [(2, 2), (3, 2), (7, 4)])
-    deal(tab, True, [(3, k) for k in range(8)], [(4, 8)])
-    deal(tab, False, [(3, k) for k in range(8)], [(6, 8)])
-    return tab
+def split_tokens(r, pairs):
+    far = {}
+    for t, pair in enumerate(pairs):
+        f = [e for e in pair if e // 32 != r // 32]
+        if len(f) == 2 or any(e // 16 == (r // 16) ^ 2 for e in f):
+            far[t] = f
+    ok = {t: [a for a in AGENTS if a in MATE_PORT or all(e % 2 == r % 2 for e in f)] for t, f in far.items()}
+    asg = {t: ok[t][(min(f) % 16 // 2) % len(ok[t])] for t, f in far.items()}
+
+    def cost():
+        dests = {a: set() for a in AGENTS}
+        for t, a in asg.items():
+            dests[a].update(far[t])
+        m = [len(d) for d in dests.values()]
+        return sum(m) + 2 * max(m)
+
+    best, better = cost(), True
+    while better:
+        better = False
+        for t in sorted(far):
+            for a in ok[t]:
+                old = asg[t]
+                if a != old:
+                    asg[t] = a
+                    c = cost()
+                    if c < best:
+                        best, better = c, True
+                    else:
+                        asg[t] = old
+    return far, asg
 
 
-AGENT = agent_table()
+def links(src, dst):
+    y, z, d = src // 8, dst // 8, (src % 8) // 4
+    if y == z or y // 32 != z // 32:
+        return None, []
+    if y % 2 != z % 2:
+        return ("mate", y, d), ([] if y ^ 1 == z else [("out", y ^ 1, d), ("in", z, d)])
+    return None, [("out", y, d), ("in", z, d)]
 
 
-def agent_of(s, d):
-    hs, cs, hd, cd = s // 16, s % 16, d // 16, d % 16
-    if hd == hs:
-        rel = 0
-    elif hd == hs ^ 1:
-        rel = 1
-    elif hd == 3 - hs:
-        rel = 2
-    else:
-        rel = 3
-    same = (cs % 2) == (cd % 2)
-    k = (((cd - cs) if same else (cd - (cs ^ 1))) // 2) % 8
-    a = AGENT[(same, rel, k)]
-    if rel == 3:
-        return True, ((3 - hs) * 16 + cs) * 8 + a
-    return False, s * 8 + a
+def choose_carriers(dirm, prxm, ptok, cap):
+    count, load = {c: 0 for c in range(NR * 8)}, {}
+
+    def book(src, dst, n):
+        count[src] += 1
+        m, sw = links(src, dst)
+        for l in ([m] if m else []) + sw:
+            load[l] = load.get(l, 0) + n
+
+    for r in range(NR):
+        count[r * 8] += 14
+    for a, ts in ptok.items():
+        book(proxy_chip(a // 8) * 8, a, len(ts))
+        book(a, proxy_chip(a // 8) * 8, len(ts))
+    for (a, e), ts in prxm.items():
+        book(a, e * 8, len(ts))
+    items, carrier = [], {}
+    for (r, e), ts in dirm.items():
+        items.append((r % 2 == e % 2, -len(ts), 0, r, e * 8))
+        items.append((r % 2 == e % 2, -len(ts), 1, e, r * 8))
+    for (a, e), ts in prxm.items():
+        if a // 8 == e:
+            carrier[(1, e, a)] = a
+        else:
+            items.append((e % 2 == (a // 8) % 2, -len(ts), 1, e, a))
+    for (same, negn, ph, y, q) in sorted(items):
+        cand = [c for c in (range(8) if same else MATE_PORT) if count[y * 8 + c] < cap]
+        if not cand:
+            return None
+
+        def score(c):
+            m, sw = links(y * 8 + c, q)
+            return (max([2 * load.get(m, 0) if m else 0] + [load.get(l, 0) for l in sw]), count[y * 8 + c], c)
+
+        c = min(cand, key=score)
+        carrier[(ph, y, q)] = y * 8 + c
+        book(y * 8 + c, q, -negn)
+    return carrier
 
 
-def layout(s, count):
-    groups = {}
-    for d in range(NR):
-        if d != s and count[d] > 0:
-            groups.setdefault(agent_of(s, d), []).append(d)
+def layout(entries, own):
     sections, col, c = [], {}, 0
-    for key in sorted(groups):
-        first, msgs = c, []
-        for d in groups[key]:
-            msgs.append((d, c, count[d]))
-            col[d] = c
-            c += count[d]
-        sections.append((key[0], key[1], first, c, msgs))
-    col[s] = c
-    return {"sections": sections, "col": col, "width": c + count[s]}
+    for (holder, q, n) in sorted(entries):
+        if not sections or sections[-1][0] != holder:
+            sections.append([holder, c, c, []])
+        sections[-1][3].append((q, c, n))
+        col[q] = c
+        c += n
+        sections[-1][2] = c
+    return {"sections": sections, "col": col, "own": c, "width": c + own}
 
 
-def slots(me, count):
+def slots(widths):
     at, c = {}, 0
-    for s in range(NR):
-        if s != me and count[s] > 0:
-            at[s] = c
-            c += (count[s] + 7) // 8 * 8
+    for key in sorted(widths):
+        at[key] = c
+        c += (widths[key] + 7) // 8 * 8
     return at, c
 
 
 def make_plan(route):
-    toks = [[[] for e in range(NR)] for r in range(NR)]
+    dirm, prxm, ptok, fars, agent = {}, {}, {}, [], []
+    self_toks = [[t for t, pair in enumerate(route[r]) if r in pair] for r in range(NR)]
     for r in range(NR):
+        far, asg = split_tokens(r, route[r])
+        fars.append(far)
+        agent.append({t: proxy_chip(r) * 8 + a for t, a in asg.items()})
         for t, pair in enumerate(route[r]):
+            if t in far:
+                ptok.setdefault(agent[r][t], []).append(t)
             for e in pair:
-                toks[r][e].append(t)
-    n = [[len(toks[r][e]) for e in range(NR)] for r in range(NR)]
-    lay1 = [layout(r, n[r]) for r in range(NR)]
-    lay2 = [layout(e, [n[r][e] for r in range(NR)]) for e in range(NR)]
-    assert max(l["width"] for l in lay2) <= LMAX and all(l["width"] == 128 for l in lay1)
-    slot1 = [slots(e, [n[r][e] for r in range(NR)]) for e in range(NR)]
-    slot2 = [slots(r, n[r]) for r in range(NR)]
-    assert max(w for at, w in slot1) <= LAND and max(w for at, w in slot2) <= RES
-    jobs = [{}, {}]
-    for ph, lays in enumerate((lay1, lay2)):
-        for s in range(NR):
-            for (relayed, core, a, b, msgs) in lays[s]["sections"]:
-                jobs[ph].setdefault(core, []).append((relayed, s, msgs))
-    return {"toks": toks, "n": n, "lay1": lay1, "lay2": lay2, "jobs": jobs,
-            "slot1": [at for at, w in slot1], "slot2": [at for at, w in slot2]}
+                if t in far and e in far[t]:
+                    prxm.setdefault((agent[r][t], e), []).append(t)
+                elif e != r:
+                    dirm.setdefault((r, e), []).append(t)
+    carrier, cap = None, 18
+    while carrier is None:
+        cap += 1
+        carrier = choose_carriers(dirm, prxm, ptok, cap)
+
+    ent1, ent2 = [[] for r in range(NR)], [[] for r in range(NR)]
+    wl, wr, wa = [{} for r in range(NR)], [{} for r in range(NR)], {a: {} for a in ptok}
+    for (r, e), ts in dirm.items():
+        ent1[r].append((carrier[(0, r, e * 8)], e * 8, len(ts)))
+        ent2[e].append((carrier[(1, e, r * 8)], r * 8, len(ts)))
+        wl[e][r * 8] = len(ts)
+        wr[r][e * 8] = len(ts)
+    for a, ts in ptok.items():
+        ent1[proxy_chip(a // 8)].append((a, a, len(ts)))
+        wr[proxy_chip(a // 8)][a] = len(ts)
+    for (a, e), ts in prxm.items():
+        ent2[e].append((carrier[(1, e, a)], a, len(ts)))
+        wl[e][a] = len(ts)
+        if a // 8 != e:
+            wa[a][e] = len(ts)
+    lay1 = [layout(ent1[r], 0) for r in range(NR)]
+    lay2 = [layout(ent2[e], len(self_toks[e])) for e in range(NR)]
+    sl, sr, sa = [slots(w) for w in wl], [slots(w) for w in wr], {a: slots(w) for a, w in wa.items()}
+    pcol = {}
+    for (a, e) in sorted(prxm):
+        pcol.setdefault(a, {"width": 0})
+        pcol[a][e] = pcol[a]["width"]
+        pcol[a]["width"] += len(prxm[(a, e)])
+    assert max(l["width"] for l in lay1) <= SEND and max(l["width"] for l in lay2) <= LMAX
+    assert max([w for at, w in sl] + [w for at, w in sa.values()]) <= LAND and max(w for at, w in sr) <= RES
+    assert max(p["width"] for p in pcol.values()) <= PSEND and max(len(ts) for ts in ptok.values()) <= POUT
+    return {"dirm": dirm, "prxm": prxm, "ptok": ptok, "far": fars, "agent": agent, "self": self_toks, "lay1": lay1,
+            "lay2": lay2, "land": [at for at, w in sl], "res": [at for at, w in sr],
+            "aland": {a: at for a, (at, w) in sa.items()}, "pcol": pcol}
 
 
 PLANS = {}
@@ -143,30 +211,90 @@ def emit(g, core, topo, T, writes):
     return len(writes)
 
 
-def agent_program(g, core, T, topo, P):
-    sent = 0
-    for ph in (0, 1):
-        jobs = P["jobs"][ph].get(core, [])
-        if not jobs:
+def messages(P, T, ph, s, core):
+    out = []
+    for (holder, a, b, msgs) in P["lay1" if ph == 0 else "lay2"][s]["sections"]:
+        if holder != core:
             continue
-        g.wait_ge(T.sem.blk1 if ph == 0 else T.sem.blk2, len(jobs))
-        writes = []
-        for (relayed, s, msgs) in jobs:
+        for (q, c, n) in msgs:
+            if q == core:
+                continue
             if ph == 0:
-                buf, out, sem = (T.rsend if relayed else T.send), T.land, T.sem.tok_in
+                at = P["land"][q // 8][s * 8]
+                out.append((T.send[:, c:c + n], T.land[:, at:at + n], q, T.sem.tok_in, n))
+            elif q % 8 == 0:
+                at = P["res"][q // 8][s * 8]
+                out.append((T.outb[:, c:c + n], T.res[:, at:at + n], q, T.sem.res_in, n))
             else:
-                buf, out, sem = (T.routb if relayed else T.outb), T.res, T.sem.res_in
-            for (d, c, n) in msgs:
-                at = (P["slot1"] if ph == 0 else P["slot2"])[d][s]
-                writes.append((buf[:, c:c + n], out[:, at:at + n], d * 8, sem, n))
+                at = P["aland"][q][s]
+                out.append((T.outb[:, c:c + n], T.land[:, at:at + n], q, T.sem.pres_in, n))
+    return out
+
+
+def blocks(P, T, ph, s):
+    out = []
+    for (holder, a, b, msgs) in P["lay1" if ph == 0 else "lay2"][s]["sections"]:
+        if holder == s * 8:
+            continue
+        if ph == 1:
+            out.append((T.outb[:, a:b], T.outb[:, a:b], holder, T.sem.blk2, b - a))
+        elif holder // 8 == s:
+            out.append((T.send[:, a:b], T.send[:, a:b], holder, T.sem.blk1, b - a))
+        else:
+            out.append((T.send[:, a:b], T.rsend[:, a:b], holder, T.sem.pblk1, b - a))
+    return out
+
+
+def helper_program(g, core, T, topo, P):
+    S, V = T.sem, g.vector
+    y, home = core // 8, proxy_chip(core // 8)
+    toks = P["ptok"].get(core, [])
+    holds = [any(sec[0] == core for sec in P[l][y]["sections"]) for l in ("lay1", "lay2")]
+    experts = sorted(e for (a, e) in P["prxm"] if a == core)
+    sent = 0
+    if holds[0]:
+        g.wait_ge(S.blk1, 1)
+        sent += emit(g, core, topo, T, messages(P, T, 0, y, core))
+    if toks:
+        base, writes, copies = P["lay1"][home]["col"][core], [], 0
+        V.wait_ge(S.pblk1, 1)
+        for e in experts:
+            ts, c = P["prxm"][(core, e)], P["pcol"][core][e]
+            for i, t in enumerate(ts):
+                k = base + toks.index(t)
+                V.tensor_copy(T.psend[:, c + i:c + i + 1], T.rsend[:, k:k + 1]).then_inc(S.repacked, 1)
+                copies += 1
+            at = P["land"][e][core]
+            writes.append((T.psend[:, c:c + len(ts)], T.land[:, at:at + len(ts)], e * 8, S.tok_in, len(ts)))
+        g.wait_ge(S.repacked, copies)
         sent += emit(g, core, topo, T, writes)
+    if holds[1]:
+        g.wait_ge(S.blk2, 1)
+        sent += emit(g, core, topo, T, messages(P, T, 1, y, core))
+    if toks:
+        if y in experts:
+            V.wait_ge(S.blk2, 1)
+        if len(experts) > (y in experts):
+            V.wait_ge(S.pres_in, len(experts) - (y in experts))
+        for i, t in enumerate(toks):
+            ins = []
+            for e in P["far"][home][t]:
+                k = P["prxm"][(core, e)].index(t)
+                if e == y:
+                    k += P["lay2"][y]["col"][core]
+                    ins.append(T.outb[:, k:k + 1])
+                else:
+                    k += P["aland"][core][e]
+                    ins.append(T.land[:, k:k + 1])
+            if len(ins) == 2:
+                V.tensor_tensor(T.pout[:, i:i + 1], ins[0], ins[1], AluOpType.add).then_inc(S.summed, 1)
+            else:
+                V.tensor_copy(T.pout[:, i:i + 1], ins[0]).then_inc(S.summed, 1)
+        g.wait_ge(S.summed, len(toks))
+        at, n = P["res"][home][core], len(toks)
+        sent += emit(g, core, topo, T, [(T.pout[:, 0:n], T.res[:, at:at + n], home * 8, S.res_in, n)])
     if sent:
-        g.wait_ge(T.sem.sent, sent)
-
-
-def blocks(lay, own, relay, sem):
-    return [(own[:, a:b], (relay if relayed else own)[:, a:b], core, sem, b - a)
-            for (relayed, core, a, b, msgs) in lay["sections"]]
+        g.wait_ge(S.sent, sent)
 
 
 def rank_program(g, core, T, topo):
@@ -174,47 +302,57 @@ def rank_program(g, core, T, topo):
     P = get_plan(route)
     r = T.rank_of(core)
     if r is None:
-        agent_program(g, core, T, topo, P)
+        helper_program(g, core, T, topo, P)
         return
     S, V, TE = T.sem, g.vector, g.tensor
-    l1, l2, n, toks = P["lay1"][r], P["lay2"][r], P["n"], P["toks"]
+    l1, l2 = P["lay1"][r], P["lay2"][r]
     g.dma_start(T.xs[:], T.x[:]).then_inc(S.ldx, 16)
     g.dma_start(T.ws[:], T.w[:]).then_inc(S.ldw, 16)
 
     V.wait_ge(S.ldx, 16)
-    n_pack = 128 - n[r][r]
-    for e in range(NR):
-        for i, t in enumerate(toks[r][e] if e != r else []):
-            c = l1["col"][e] + i
-            V.tensor_copy(T.send[:, c:c + 1], T.xs[:, t:t + 1]).then_inc(S.packed, 1)
-    g.wait_ge(S.packed, n_pack)
-    sent = emit(g, core, topo, T, blocks(l1, T.send, T.rsend, S.blk1))
+    for (q, c) in sorted(l1["col"].items()):
+        ts = P["dirm"][(r, q // 8)] if q % 8 == 0 else P["ptok"][q]
+        for i, t in enumerate(ts):
+            V.tensor_copy(T.send[:, c + i:c + i + 1], T.xs[:, t:t + 1]).then_inc(S.packed, 1)
+    g.wait_ge(S.packed, l1["width"])
+    sent = emit(g, core, topo, T, blocks(P, T, 0, r) + messages(P, T, 0, r, core))
 
-    senders = [s for s in range(NR) if s != r and n[s][r]]
-    W = l2["width"]
+    peers = sorted(P["land"][r])
     TE.wait_ge(S.ldw, 16)
     TE.wait_ge(S.ldx, 16)
-    TE.wait_ge(S.tok_in, len(senders))
-    for s in senders:
-        a, c, k = P["slot1"][r][s], l2["col"][s], n[s][r]
-        TE.matmul(T.acc[:, c:c + k], T.ws[:], T.land[:, a:a + k], True, True).then_inc(S.mm, 1)
-    for i, t in enumerate(toks[r][r]):
-        c = l2["col"][r] + i
+    TE.wait_ge(S.tok_in, len(peers))
+    for q in peers:
+        n = len(P["dirm"][(q // 8, r)] if q % 8 == 0 else P["prxm"][(q, r)])
+        a, c = P["land"][r][q], l2["col"][q]
+        TE.matmul(T.acc[:, c:c + n], T.ws[:], T.land[:, a:a + n], True, True).then_inc(S.mm, 1)
+    for i, t in enumerate(P["self"][r]):
+        c = l2["own"] + i
         TE.matmul(T.acc[:, c:c + 1], T.ws[:], T.xs[:, t:t + 1], True, True).then_inc(S.mm, 1)
-    V.wait_ge(S.mm, len(senders) + n[r][r])
+    W = l2["width"]
+    V.wait_ge(S.mm, len(peers) + len(P["self"][r]))
     V.tensor_copy(T.outb[:, 0:W], T.acc[:, 0:W]).then_inc(S.cast, 1)
     g.wait_ge(S.cast, 1)
-    sent += emit(g, core, topo, T, blocks(l2, T.outb, T.routb, S.blk2))
+    sent += emit(g, core, topo, T, blocks(P, T, 1, r) + messages(P, T, 1, r, core))
 
-    n_back = sum(1 for e in range(NR) if e != r and n[r][e])
     V.wait_ge(S.cast, 1)
-    V.wait_ge(S.res_in, n_back)
+    V.wait_ge(S.res_in, len(P["res"][r]))
     for t, pair in enumerate(route[r]):
         ins = []
+        if t in P["far"][r]:
+            a = P["agent"][r][t]
+            k = P["res"][r][a] + P["ptok"][a].index(t)
+            ins.append(T.res[:, k:k + 1])
         for e in pair:
-            c = (l2["col"][r] if e == r else P["slot2"][r][e]) + toks[r][e].index(t)
-            ins.append((T.outb if e == r else T.res)[:, c:c + 1])
-        V.tensor_tensor(T.ys[:, t:t + 1], ins[0], ins[1], AluOpType.add).then_inc(S.added, 1)
+            if e == r:
+                k = l2["own"] + P["self"][r].index(t)
+                ins.append(T.outb[:, k:k + 1])
+            elif not (t in P["far"][r] and e in P["far"][r][t]):
+                k = P["res"][r][e * 8] + P["dirm"][(r, e)].index(t)
+                ins.append(T.res[:, k:k + 1])
+        if len(ins) == 2:
+            V.tensor_tensor(T.ys[:, t:t + 1], ins[0], ins[1], AluOpType.add).then_inc(S.added, 1)
+        else:
+            V.tensor_copy(T.ys[:, t:t + 1], ins[0]).then_inc(S.added, 1)
     g.wait_ge(S.added, 64)
     g.dma_start(T.y[:], T.ys[:]).then_inc(S.stored, 16)
     g.wait_ge(S.stored, 16)

@@ -4,6 +4,7 @@ from concourse.mybir import AluOpType
 NR = 64
 MATE_PORT = (2, 3, 6, 7)
 AGENTS = (4, 5, 3, 7)
+CARRIERS = ((0, 1, 2, 6), (1, 2, 3, 4, 5, 6, 7))
 SEND, LMAX, LAND, RES, PSEND, POUT = 120, 160, 600, 392, 40, 24
 
 SCRATCH = {
@@ -78,7 +79,7 @@ def choose_carriers(dirm, prxm, ptok, cap):
             load[l] = load.get(l, 0) + n
 
     for r in range(NR):
-        count[r * 8] += 14
+        count[r * 8] += sum(1 for cs in CARRIERS for c in cs if c)
     for a, ts in ptok.items():
         book(proxy_chip(a // 8) * 8, a, len(ts))
         book(a, proxy_chip(a // 8) * 8, len(ts))
@@ -94,7 +95,7 @@ def choose_carriers(dirm, prxm, ptok, cap):
         else:
             items.append((e % 2 == (a // 8) % 2, -len(ts), 1, e, a))
     for (same, negn, ph, y, q) in sorted(items):
-        cand = [c for c in (range(8) if same else MATE_PORT) if count[y * 8 + c] < cap]
+        cand = [c for c in CARRIERS[ph] if (same or c in MATE_PORT) and count[y * 8 + c] < cap]
         if not cand:
             return None
 

from concourse.bass import RemoteDMATransfer, DstId
from concourse.mybir import AluOpType

NR = 64
MATE_PORT = (2, 3, 6, 7)
AGENTS = (4, 5, 3, 7)
CARRIERS = ((0, 1, 2, 6), (1, 2, 3, 4, 5, 6, 7))
SEND, LMAX, LAND, RES, PSEND, POUT = 120, 160, 600, 392, 40, 24

SCRATCH = {
    "xs": ("sbuf", [128, 64], "bfloat16"),
    "ws": ("sbuf", [128, 128], "bfloat16"),
    "send": ("sbuf", [128, SEND], "bfloat16"),
    "rsend": ("sbuf", [128, SEND], "bfloat16"),
    "psend": ("sbuf", [128, PSEND], "bfloat16"),
    "land": ("sbuf", [128, LAND], "bfloat16"),
    "acc": ("psum", [128, LMAX], "float32"),
    "outb": ("sbuf", [128, LMAX], "bfloat16"),
    "pout": ("sbuf", [128, POUT], "bfloat16"),
    "res": ("sbuf", [128, RES], "bfloat16"),
    "ys": ("sbuf", [128, 64], "bfloat16"),
}
SEMAPHORES = ["ldx", "ldw", "packed", "blk1", "pblk1", "repacked", "tok_in", "mm", "cast", "blk2", "pres_in", "summed",
              "res_in", "added", "stored", "sent"]


def proxy_chip(r):
    return (3 - r // 16) * 16 + r % 16


def split_tokens(r, pairs):
    far = {}
    for t, pair in enumerate(pairs):
        f = [e for e in pair if e // 32 != r // 32]
        if len(f) == 2 or any(e // 16 == (r // 16) ^ 2 for e in f):
            far[t] = f
    ok = {t: [a for a in AGENTS if a in MATE_PORT or all(e % 2 == r % 2 for e in f)] for t, f in far.items()}
    asg = {t: ok[t][(min(f) % 16 // 2) % len(ok[t])] for t, f in far.items()}

    def cost():
        dests = {a: set() for a in AGENTS}
        for t, a in asg.items():
            dests[a].update(far[t])
        m = [len(d) for d in dests.values()]
        return sum(m) + 2 * max(m)

    best, better = cost(), True
    while better:
        better = False
        for t in sorted(far):
            for a in ok[t]:
                old = asg[t]
                if a != old:
                    asg[t] = a
                    c = cost()
                    if c < best:
                        best, better = c, True
                    else:
                        asg[t] = old
    return far, asg


def links(src, dst):
    y, z, d = src // 8, dst // 8, (src % 8) // 4
    if y == z or y // 32 != z // 32:
        return None, []
    if y % 2 != z % 2:
        return ("mate", y, d), ([] if y ^ 1 == z else [("out", y ^ 1, d), ("in", z, d)])
    return None, [("out", y, d), ("in", z, d)]


def choose_carriers(dirm, prxm, ptok, cap):
    count, load = {c: 0 for c in range(NR * 8)}, {}

    def book(src, dst, n):
        count[src] += 1
        m, sw = links(src, dst)
        for l in ([m] if m else []) + sw:
            load[l] = load.get(l, 0) + n

    for r in range(NR):
        count[r * 8] += sum(1 for cs in CARRIERS for c in cs if c)
    for a, ts in ptok.items():
        book(proxy_chip(a // 8) * 8, a, len(ts))
        book(a, proxy_chip(a // 8) * 8, len(ts))
    for (a, e), ts in prxm.items():
        book(a, e * 8, len(ts))
    items, carrier = [], {}
    for (r, e), ts in dirm.items():
        items.append((r % 2 == e % 2, -len(ts), 0, r, e * 8))
        items.append((r % 2 == e % 2, -len(ts), 1, e, r * 8))
    for (a, e), ts in prxm.items():
        if a // 8 == e:
            carrier[(1, e, a)] = a
        else:
            items.append((e % 2 == (a // 8) % 2, -len(ts), 1, e, a))
    for (same, negn, ph, y, q) in sorted(items):
        cand = [c for c in CARRIERS[ph] if (same or c in MATE_PORT) and count[y * 8 + c] < cap]
        if not cand:
            return None

        def score(c):
            m, sw = links(y * 8 + c, q)
            return (max([2 * load.get(m, 0) if m else 0] + [load.get(l, 0) for l in sw]), count[y * 8 + c], c)

        c = min(cand, key=score)
        carrier[(ph, y, q)] = y * 8 + c
        book(y * 8 + c, q, -negn)
    return carrier


def layout(entries, own):
    sections, col, c = [], {}, 0
    for (holder, q, n) in sorted(entries):
        if not sections or sections[-1][0] != holder:
            sections.append([holder, c, c, []])
        sections[-1][3].append((q, c, n))
        col[q] = c
        c += n
        sections[-1][2] = c
    return {"sections": sections, "col": col, "own": c, "width": c + own}


def slots(widths):
    at, c = {}, 0
    for key in sorted(widths):
        at[key] = c
        c += (widths[key] + 7) // 8 * 8
    return at, c


def make_plan(route):
    dirm, prxm, ptok, fars, agent = {}, {}, {}, [], []
    self_toks = [[t for t, pair in enumerate(route[r]) if r in pair] for r in range(NR)]
    for r in range(NR):
        far, asg = split_tokens(r, route[r])
        fars.append(far)
        agent.append({t: proxy_chip(r) * 8 + a for t, a in asg.items()})
        for t, pair in enumerate(route[r]):
            if t in far:
                ptok.setdefault(agent[r][t], []).append(t)
            for e in pair:
                if t in far and e in far[t]:
                    prxm.setdefault((agent[r][t], e), []).append(t)
                elif e != r:
                    dirm.setdefault((r, e), []).append(t)
    carrier, cap = None, 18
    while carrier is None:
        cap += 1
        carrier = choose_carriers(dirm, prxm, ptok, cap)

    ent1, ent2 = [[] for r in range(NR)], [[] for r in range(NR)]
    wl, wr, wa = [{} for r in range(NR)], [{} for r in range(NR)], {a: {} for a in ptok}
    for (r, e), ts in dirm.items():
        ent1[r].append((carrier[(0, r, e * 8)], e * 8, len(ts)))
        ent2[e].append((carrier[(1, e, r * 8)], r * 8, len(ts)))
        wl[e][r * 8] = len(ts)
        wr[r][e * 8] = len(ts)
    for a, ts in ptok.items():
        ent1[proxy_chip(a // 8)].append((a, a, len(ts)))
        wr[proxy_chip(a // 8)][a] = len(ts)
    for (a, e), ts in prxm.items():
        ent2[e].append((carrier[(1, e, a)], a, len(ts)))
        wl[e][a] = len(ts)
        if a // 8 != e:
            wa[a][e] = len(ts)
    lay1 = [layout(ent1[r], 0) for r in range(NR)]
    lay2 = [layout(ent2[e], len(self_toks[e])) for e in range(NR)]
    sl, sr, sa = [slots(w) for w in wl], [slots(w) for w in wr], {a: slots(w) for a, w in wa.items()}
    pcol = {}
    for (a, e) in sorted(prxm):
        pcol.setdefault(a, {"width": 0})
        pcol[a][e] = pcol[a]["width"]
        pcol[a]["width"] += len(prxm[(a, e)])
    assert max(l["width"] for l in lay1) <= SEND and max(l["width"] for l in lay2) <= LMAX
    assert max([w for at, w in sl] + [w for at, w in sa.values()]) <= LAND and max(w for at, w in sr) <= RES
    assert max(p["width"] for p in pcol.values()) <= PSEND and max(len(ts) for ts in ptok.values()) <= POUT
    return {"dirm": dirm, "prxm": prxm, "ptok": ptok, "far": fars, "agent": agent, "self": self_toks, "lay1": lay1,
            "lay2": lay2, "land": [at for at, w in sl], "res": [at for at, w in sr],
            "aland": {a: at for a, (at, w) in sa.items()}, "pcol": pcol}


PLANS = {}


def get_plan(route):
    if "p" not in PLANS:
        PLANS["p"] = make_plan(route)
    return PLANS["p"]


def emit(g, core, topo, T, writes):
    by_width = {}
    for w in writes:
        by_width.setdefault(w[4], []).append(w)
    for width in sorted(by_width):
        ws = by_width[width]
        for i in range(0, len(ws), 8):
            chunk = ws[i:i + 8]
            if len(chunk) == 1:
                src, dst, dcore, sem, wd = chunk[0]
                rid, pid = topo.addr(dcore, core)
                g.remote_dma(out_ap=dst, in_ap=src, remote_sem=sem, local_sem=T.sem.sent, pid=pid, routing_id=rid,
                             dma_engine_mask=1)
                continue
            trs = []
            for j, (src, dst, dcore, sem, wd) in enumerate(chunk):
                rid, pid = topo.addr(dcore, core)
                trs.append(RemoteDMATransfer(dst_ids=[DstId(rid=rid, pnc=pid)], dma_engine_mask=1 << j, remote_sem=sem,
                                             src=src, dst=dst))
            g.remote_dma_fused(trs, local_sem=T.sem.sent)
    return len(writes)


def messages(P, T, ph, s, core):
    out = []
    for (holder, a, b, msgs) in P["lay1" if ph == 0 else "lay2"][s]["sections"]:
        if holder != core:
            continue
        for (q, c, n) in msgs:
            if q == core:
                continue
            if ph == 0:
                at = P["land"][q // 8][s * 8]
                out.append((T.send[:, c:c + n], T.land[:, at:at + n], q, T.sem.tok_in, n))
            elif q % 8 == 0:
                at = P["res"][q // 8][s * 8]
                out.append((T.outb[:, c:c + n], T.res[:, at:at + n], q, T.sem.res_in, n))
            else:
                at = P["aland"][q][s]
                out.append((T.outb[:, c:c + n], T.land[:, at:at + n], q, T.sem.pres_in, n))
    return out


def blocks(P, T, ph, s):
    out = []
    for (holder, a, b, msgs) in P["lay1" if ph == 0 else "lay2"][s]["sections"]:
        if holder == s * 8:
            continue
        if ph == 1:
            out.append((T.outb[:, a:b], T.outb[:, a:b], holder, T.sem.blk2, b - a))
        elif holder // 8 == s:
            out.append((T.send[:, a:b], T.send[:, a:b], holder, T.sem.blk1, b - a))
        else:
            out.append((T.send[:, a:b], T.rsend[:, a:b], holder, T.sem.pblk1, b - a))
    return out


def helper_program(g, core, T, topo, P):
    S, V = T.sem, g.vector
    y, home = core // 8, proxy_chip(core // 8)
    toks = P["ptok"].get(core, [])
    holds = [any(sec[0] == core for sec in P[l][y]["sections"]) for l in ("lay1", "lay2")]
    experts = sorted(e for (a, e) in P["prxm"] if a == core)
    sent = 0
    if holds[0]:
        g.wait_ge(S.blk1, 1)
        sent += emit(g, core, topo, T, messages(P, T, 0, y, core))
    if toks:
        base, writes, copies = P["lay1"][home]["col"][core], [], 0
        V.wait_ge(S.pblk1, 1)
        for e in experts:
            ts, c = P["prxm"][(core, e)], P["pcol"][core][e]
            for i, t in enumerate(ts):
                k = base + toks.index(t)
                V.tensor_copy(T.psend[:, c + i:c + i + 1], T.rsend[:, k:k + 1]).then_inc(S.repacked, 1)
                copies += 1
            at = P["land"][e][core]
            writes.append((T.psend[:, c:c + len(ts)], T.land[:, at:at + len(ts)], e * 8, S.tok_in, len(ts)))
        g.wait_ge(S.repacked, copies)
        sent += emit(g, core, topo, T, writes)
    if holds[1]:
        g.wait_ge(S.blk2, 1)
        sent += emit(g, core, topo, T, messages(P, T, 1, y, core))
    if toks:
        if y in experts:
            V.wait_ge(S.blk2, 1)
        if len(experts) > (y in experts):
            V.wait_ge(S.pres_in, len(experts) - (y in experts))
        for i, t in enumerate(toks):
            ins = []
            for e in P["far"][home][t]:
                k = P["prxm"][(core, e)].index(t)
                if e == y:
                    k += P["lay2"][y]["col"][core]
                    ins.append(T.outb[:, k:k + 1])
                else:
                    k += P["aland"][core][e]
                    ins.append(T.land[:, k:k + 1])
            if len(ins) == 2:
                V.tensor_tensor(T.pout[:, i:i + 1], ins[0], ins[1], AluOpType.add).then_inc(S.summed, 1)
            else:
                V.tensor_copy(T.pout[:, i:i + 1], ins[0]).then_inc(S.summed, 1)
        g.wait_ge(S.summed, len(toks))
        at, n = P["res"][home][core], len(toks)
        sent += emit(g, core, topo, T, [(T.pout[:, 0:n], T.res[:, at:at + n], home * 8, S.res_in, n)])
    if sent:
        g.wait_ge(S.sent, sent)


def rank_program(g, core, T, topo):
    route = T.tables["ROUTE"]
    P = get_plan(route)
    r = T.rank_of(core)
    if r is None:
        helper_program(g, core, T, topo, P)
        return
    S, V, TE = T.sem, g.vector, g.tensor
    l1, l2 = P["lay1"][r], P["lay2"][r]
    g.dma_start(T.xs[:], T.x[:]).then_inc(S.ldx, 16)
    g.dma_start(T.ws[:], T.w[:]).then_inc(S.ldw, 16)

    V.wait_ge(S.ldx, 16)
    for (q, c) in sorted(l1["col"].items()):
        ts = P["dirm"][(r, q // 8)] if q % 8 == 0 else P["ptok"][q]
        for i, t in enumerate(ts):
            V.tensor_copy(T.send[:, c + i:c + i + 1], T.xs[:, t:t + 1]).then_inc(S.packed, 1)
    g.wait_ge(S.packed, l1["width"])
    sent = emit(g, core, topo, T, blocks(P, T, 0, r) + messages(P, T, 0, r, core))

    peers = sorted(P["land"][r])
    TE.wait_ge(S.ldw, 16)
    TE.wait_ge(S.ldx, 16)
    TE.wait_ge(S.tok_in, len(peers))
    for q in peers:
        n = len(P["dirm"][(q // 8, r)] if q % 8 == 0 else P["prxm"][(q, r)])
        a, c = P["land"][r][q], l2["col"][q]
        TE.matmul(T.acc[:, c:c + n], T.ws[:], T.land[:, a:a + n], True, True).then_inc(S.mm, 1)
    for i, t in enumerate(P["self"][r]):
        c = l2["own"] + i
        TE.matmul(T.acc[:, c:c + 1], T.ws[:], T.xs[:, t:t + 1], True, True).then_inc(S.mm, 1)
    W = l2["width"]
    V.wait_ge(S.mm, len(peers) + len(P["self"][r]))
    V.tensor_copy(T.outb[:, 0:W], T.acc[:, 0:W]).then_inc(S.cast, 1)
    g.wait_ge(S.cast, 1)
    sent += emit(g, core, topo, T, blocks(P, T, 1, r) + messages(P, T, 1, r, core))

    V.wait_ge(S.cast, 1)
    V.wait_ge(S.res_in, len(P["res"][r]))
    for t, pair in enumerate(route[r]):
        ins = []
        if t in P["far"][r]:
            a = P["agent"][r][t]
            k = P["res"][r][a] + P["ptok"][a].index(t)
            ins.append(T.res[:, k:k + 1])
        for e in pair:
            if e == r:
                k = l2["own"] + P["self"][r].index(t)
                ins.append(T.outb[:, k:k + 1])
            elif not (t in P["far"][r] and e in P["far"][r][t]):
                k = P["res"][r][e * 8] + P["dirm"][(r, e)].index(t)
                ins.append(T.res[:, k:k + 1])
        if len(ins) == 2:
            V.tensor_tensor(T.ys[:, t:t + 1], ins[0], ins[1], AluOpType.add).then_inc(S.added, 1)
        else:
            V.tensor_copy(T.ys[:, t:t + 1], ins[0]).then_inc(S.added, 1)
    g.wait_ge(S.added, 64)
    g.dma_start(T.y[:], T.ys[:]).then_inc(S.stored, 16)
    g.wait_ge(S.stored, 16)
    g.wait_ge(S.sent, sent)
